import numpy as np
import ml_dtypes


def mxq(x, axis, fmt="e4m3"):
    dtype, down = {"e4m3": (ml_dtypes.float8_e4m3fn, 7), "e5m2": (ml_dtypes.float8_e5m2, 14)}[fmt]
    v = np.moveaxis(np.asarray(x, np.float32).astype(ml_dtypes.bfloat16).astype(np.float64), axis, -1)
    blocks = v.reshape(v.shape[:-1] + (-1, 32))
    amax = np.abs(blocks).max(-1, keepdims=True)
    byte = np.maximum(np.where(amax > 0, np.frexp(amax)[1] - 1 + 127, 0) - down, 1)
    scale = np.exp2(byte - 127.0)
    codes = (blocks / scale).astype(np.float32).astype(dtype).astype(np.float64)
    return np.moveaxis((codes * scale).reshape(v.shape), -1, axis)


WIDE = False


def mx_kscale(k):
    if not WIDE:
        return np.ones(k)
    levels = np.array([10, -10, 5, -5, 0])
    if k % 512:
        return np.exp2(np.random.permutation(np.resize(levels, k // 32))).repeat(32)
    a = np.empty((k // 512, 16))
    for p in range(k // 512):
        a[p, :8] = np.random.permutation(np.resize(levels, 8))
        for g in range(8):
            far = levels[np.abs(levels - a[p, g]) >= 10]
            a[p, g + 8] = far[np.random.randint(len(far))]
    return np.exp2(a.ravel()).repeat(32)


def f64(x):
    return np.asarray(x).astype(np.float64)


def striped(idx):
    return np.tile(np.asarray(idx).reshape(-1, 16).T, (8, 1)).astype(np.uint16)


def unstriped(offs):
    return offs[:16].T.reshape(-1).astype(np.int64)


E2M1 = np.array([0.0, 0.5, 1.0, 1.5, 2.0, 3.0, 4.0, 6.0, -0.0, -0.5, -1.0, -1.5, -2.0, -3.0, -4.0, -6.0])


def pack_weight(w, fmt):
    k, n = w.shape
    w = f64(np.asarray(w, np.float32).astype(ml_dtypes.bfloat16)).reshape(k // 32, 32, n)
    amax = np.abs(w).max(1)
    if fmt == "e4m3":
        byte = np.frexp(amax)[1] - 1 + 127 - 7
    else:
        mant, ex = np.frexp(amax / 6.0)
        byte = np.where(mant > 0.5, ex, ex - 1) + 127
    byte = np.clip(np.where(amax > 0, byte, 1), 1, 254)
    scaled = (w * np.exp2(127.0 - byte)[:, None, :]).reshape(k, n).astype(np.float32)
    by_word = np.ascontiguousarray(scaled.reshape(k // 512, 128, 4, n).transpose(0, 1, 3, 2))
    if fmt == "e4m3":
        words = by_word.astype(ml_dtypes.float8_e4m3fn).view(np.uint8)
    else:
        c = by_word.astype(ml_dtypes.float4_e2m1fn).view(np.uint8) & 0xF
        words = (c[..., 0::2] | (c[..., 1::2] << 4)).reshape(k // 512, 128, 2 * n)
    return np.ascontiguousarray(words), np.ascontiguousarray(byte.astype(np.uint8).reshape(k // 512, 16, n))


def unpack_weight(words, scales, fmt):
    g, _, n = scales.shape
    words = np.ascontiguousarray(words).reshape(g, 128, n, -1)
    if fmt == "e4m3":
        vals = words.view(ml_dtypes.float8_e4m3fn).astype(np.float64)
    else:
        nib = np.empty((g, 128, n, 4), np.uint8)
        nib[..., 0::2] = words & 0xF
        nib[..., 1::2] = words >> 4
        vals = E2M1[nib]
    vals = vals * np.repeat(np.exp2(scales.astype(np.float64) - 127.0), 8, axis=1)[..., None]
    return vals.transpose(0, 1, 3, 2).reshape(g * 512, n)


K, T, I, C, J, N = 512, 1024, 512, 1024, 512, 512


def setup_inputs():
    n = np.random.standard_normal
    idx = np.random.permutation(C)[:J]
    idx2 = np.random.permutation(T)[:I]
    fk = mx_kscale(K)
    fj = mx_kscale(J)
    xtp = pack_weight(n((K, T)) * np.random.uniform(0.2, 2.0, (1, T)) / fk[:, None], "e2m1")
    wcp = pack_weight(n((K, C)) * 1 / np.sqrt(K) * fk[:, None], "e4m3")
    wop = pack_weight(n((J, N)) * 1 / np.sqrt(J) / fj[:, None], "e2m1")
    return {
        "xt_words": xtp[0],
        "xt_scales": xtp[1],
        "wc_words": wcp[0],
        "wc_scales": wcp[1],
        "fj": (np.random.uniform(0.5, 2.0, (J, 1)) * fj[:, None]).astype(np.float32),
        "wo_words": wop[0],
        "wo_scales": wop[1],
        "offs": striped(idx),
        "offs2": striped(idx2),
    }


def reference(xt_words, xt_scales, wc_words, wc_scales, fj, wo_words, wo_scales, offs, offs2):
    idx = unstriped(offs)
    idx2 = unstriped(offs2)
    xtu = unpack_weight(xt_words, xt_scales, "e2m1")
    wcu = unpack_weight(wc_words, wc_scales, "e4m3")
    wou = unpack_weight(wo_words, wo_scales, "e2m1")
    xtidx2g = xtu[:, idx2]
    z = xtidx2g.T @ wcu
    u = z * 1.0 / np.sqrt(np.mean(np.square(z), axis=1, keepdims=True) + 0.01)
    us1 = u[:, idx]
    ut = us1.T
    uw = ut * f64(fj)
    uwq = mxq(uw, 0, "e4m3")
    y = wou.T @ uwq
    return y

@@ -1,0 +1,204 @@
+from contextlib import ExitStack
+
+import concourse.mybir as mybir
+from concourse.masks import make_identity
+
+K, T, I, C, J, N = 512, 1024, 512, 1024, 512, 512
+P = 128
+PACK = 4
+BANK = 512
+TILES = I // P
+EPS = 0.01
+
+F32 = mybir.dt.float32
+BF16 = mybir.dt.bfloat16
+I32 = mybir.dt.int32
+U32 = mybir.dt.uint32
+U16 = mybir.dt.uint16
+U8 = mybir.dt.uint8
+FP8X4 = mybir.dt.float8_e4m3fn_x4
+FP4X4 = mybir.dt.float4_e2m1fn_x4
+ACT = mybir.ActivationFunctionType
+ALU = mybir.AluOpType
+
+FLOPS = 2 * K * I * C + 2 * J * N * I
+
+
+def load_scales(queue, plane, rows, q):
+    width = rows.shape[2] // 4
+    src = rows[0, 4 * q : 4 * q + 4, :].bitcast(I32).unsqueeze(0).to_broadcast([8, 4, width])
+    queue.dma_start(out=plane[32 * q : 32 * q + 32, :].bitcast(I32), in_=src)
+
+
+def tile_list_unit_rows_listed_features_kernel(
+    tc, xt_words, xt_scales, wc_words, wc_scales, fj, wo_words, wo_scales, offs, offs2, out
+):
+    nc = tc.nc
+    with ExitStack() as ctx:
+        keep = ctx.enter_context(tc.tile_pool(name="keep", bufs=1))
+        rows = ctx.enter_context(tc.tile_pool(name="rows", bufs=1))
+        psum = ctx.enter_context(tc.psum_pool(name="psum", bufs=1))
+
+        token_list = keep.tile([P, I // 16], U16, name="token_list")
+        feature_list = keep.tile([P, J // 16], U16, name="feature_list")
+        x_words = keep.tile([P, T], U16, name="x_words", align_bytes=64)
+        x_plane = keep.tile([P, T], U8, name="x_plane", align_bytes=64)
+        wc_sb = keep.tile([P, C], U32, name="wc_sb", align_bytes=64)
+        wc_plane = keep.tile([P, C], U8, name="wc_plane", align_bytes=64)
+        wo_sb = keep.tile([P, 2 * N], U8, name="wo_sb", align_bytes=64)
+        wo_plane = keep.tile([P, N], U8, name="wo_plane", align_bytes=64)
+        fj_sb = keep.tile([P, PACK], F32, name="fj_sb")
+        ident = keep.tile([P, P], F32, name="ident")
+        warm = keep.tile([P, 2], F32, name="warm")
+
+
+        wc_flat = wc_words[0].rearrange("p n t -> p (n t)").bitcast(I32)
+        nc.sync.dma_start(token_list[:], offs2)
+        load_scales(nc.scalar, wc_plane, wc_scales, 0)
+        load_scales(nc.sync, x_plane, xt_scales, 0)
+        nc.scalar.dma_start(out=x_words[:].bitcast(I32), in_=xt_words[0].bitcast(I32))
+        load_scales(nc.sync, x_plane, xt_scales, 1)
+        load_scales(nc.scalar, x_plane, xt_scales, 2)
+        load_scales(nc.sync, x_plane, xt_scales, 3)
+        nc.scalar.dma_start(out=wc_sb[:].bitcast(I32), in_=wc_flat)
+        for q in range(1, 4):
+            load_scales(nc.sync, wc_plane, wc_scales, q)
+        nc.sync.dma_start(feature_list[:], offs)
+        nc.sync.dma_start(out=fj_sb[:], in_=fj.rearrange("(p t) o -> p (t o)", t=PACK))
+        nc.sync.dma_start(out=wo_sb[:].bitcast(I32), in_=wo_words[0].bitcast(I32))
+        for q in range(4):
+            load_scales(nc.sync, wo_plane, wo_scales, q)
+
+        nc.gpsimd.memset(warm[:, 0:1], 1.0)
+        nc.scalar.activation(warm[:, 1:2], warm[:, 0:1], ACT.Abs_reciprocal_sqrt)
+        make_identity(nc, ident[:])
+
+        z = []
+        for first, count in ((0, 1), (1, 1), (2, 2)):
+            cols = slice(first * 8, (first + count) * 8)
+            xg_words = keep.tile([P, count * P], U16, name=f"xg_words{first}", align_bytes=64)
+            xg_plane = keep.tile([P, count * P], U8, name=f"xg_plane{first}", align_bytes=64)
+            nc.vector.tensor_copy(xg_words[:], x_words[:].indirect(token_list[:, cols]))
+            nc.vector.tensor_copy(xg_plane[:], x_plane[:].indirect(token_list[:, cols]))
+            for s in range(count):
+                pair = []
+                for h in range(2):
+                    bank = psum.tile([P, BANK], F32, name=f"z{first + s}{h}", tag=f"bank{2 * (first + s) + h}")
+                    pair.append(bank)
+                    nc.tensor.matmul_mx(
+                        out=bank[:],
+                        lhsT=xg_words[:, s * P : (s + 1) * P].bitcast(FP4X4),
+                        lhsT_scale=xg_plane[:, s * P : (s + 1) * P],
+                        rhs=wc_sb[:, h * BANK : (h + 1) * BANK].bitcast(FP8X4),
+                        rhs_scale=wc_plane[:, h * BANK : (h + 1) * BANK],
+                        start=True,
+                        stop=True,
+                    )
+                z.append(pair)
+
+        halves = [slice(h * BANK, (h + 1) * BANK) for h in range(2)]
+        u = [rows.tile([P, C], F32, name=f"u{i}", align_bytes=64, offset=4 * C * i) for i in range(TILES)]
+        rstd = {}
+        later = {}
+        picked = {}
+
+        def row_scale(i):
+            r = keep.tile([P, 1], F32, name=f"rstd{i}", tag=f"rstd{max(i - 1, 0)}")
+            stat = keep.tile([P, 4], F32, name=f"stat{i}", tag=f"stat{i % 2}")
+            if i == 1:
+                moments = keep.tile([P, 16], F32, name="moments", tag="g0")
+                for h in range(2):
+                    nc.vector.bn_stats(moments[:, 6 * h : 6 * h + 6], z[i][h][:])
+                nc.vector.bn_aggr(moments[:, 12:14], moments[:, 0:12])
+                nc.vector.scalar_tensor_tensor(
+                    stat[:, 0:1], moments[:, 12:13], moments[:, 12:13], moments[:, 13:14], ALU.mult, ALU.add
+                )
+                nc.scalar.activation(r[:], stat[:, 0:1], ACT.Abs_reciprocal_sqrt, bias=EPS)
+            else:
+                for h in range(2):
+                    nc.scalar.activation(
+                        u[i][:, halves[h]], z[i][h][:], ACT.Square, scale=1.0 / 32.0, accum_out=stat[:, h : h + 1]
+                    )
+                nc.scalar.activation(stat[:, 2:3], stat[:, 0:1], ACT.Identity, bias=EPS)
+                nc.scalar.activation(r[:], stat[:, 1:2], ACT.Abs_reciprocal_sqrt, bias=stat[:, 2:3])
+            rstd[i] = r
+
+        def pick(i):
+            r = rstd[i]
+            if i in (0, 1):
+                nc.vector.tensor_scalar(u[i][:, halves[0]], z[i][0][:], r[:], None, ALU.mult)
+                nc.scalar.activation(u[i][:, halves[1]], z[i][1][:], ACT.Copy, scale=r[:])
+            elif True:
+                for h in range(2):
+                    nc.scalar.activation(u[i][:, halves[h]], z[i][h][:], ACT.Copy, scale=r[:])
+            else:
+                nc.scalar.activation(u[i][:], z[i][:], ACT.Copy, scale=r[:])
+            g = keep.tile([P, J], F32, name=f"picked{i}", tag=f"g{i}")
+            nc.vector.tensor_copy(g[:], u[i][:].indirect(feature_list[:]))
+            picked[i] = g
+
+        def turn(i):
+            g = picked[i]
+            pair = psum.tile([P, PACK, P], F32, name=f"t{i}", tag=f"bank{2 * i if i < TILES - 1 else 1}")
+            by_slot = g[:].rearrange("p (q t) -> p t q", t=PACK)
+            for t in range(PACK):
+                nc.tensor.transpose(pair[:, t, :], by_slot[:, t, :], ident[:])
+            later[i] = pair
+
+        def second(i):
+            pair = later[i]
+            uw = rows.tile([P, P, PACK], BF16, name=f"uw{i}", align_bytes=64, offset=4 * C * (i + 1))
+            nc.vector.tensor_tensor(
+                uw[:],
+                pair[:].rearrange("p t i -> p i t"),
+                fj_sb[:].unsqueeze(1).to_broadcast([P, P, PACK]),
+                ALU.mult,
+            )
+            if i == 1:
+                codes = rows.tile([P, P], U32, name="codes1", align_bytes=64, offset=4 * C * 3 + 2 * J)
+            else:
+                codes = keep.tile([P, P], U32, name=f"codes{i}", align_bytes=64)
+            plane = keep.tile([P, P], U8, name=f"plane{i}", align_bytes=64)
+            nc.vector.quantize_mx(
+                out=codes[:].bitcast(FP8X4), scales=plane[:], in_=uw[:].rearrange("p i t -> p (i t)")
+            )
+            last = i == TILES - 1
+            out_view = out.rearrange("(a p) i -> p a i", p=P)[:, :, i * P : (i + 1) * P]
+            for part in range(2 if last else 1):
+                blocks = range(2 * part, 2 * part + 2) if last else range(4)
+                bank = psum.tile([P, PACK, P], F32, name=f"o{i}_{part}", tag=f"bank{2 * i + 1 - part}")
+                for a in blocks:
+                    nc.tensor.matmul_mx(
+                        out=bank[:, a, :],
+                        lhsT=wo_sb[:, 2 * a * P : 2 * (a + 1) * P].bitcast(FP4X4),
+                        lhsT_scale=wo_plane[:, a * P : (a + 1) * P],
+                        rhs=codes[:].bitcast(FP8X4),
+                        rhs_scale=plane[:],
+                        start=True,
+                        stop=True,
+                    )
+                span = slice(blocks.start, blocks.stop)
+                y = keep.tile([P, len(blocks), P], F32, name=f"y{i}_{part}", tag="rstd2" if i == 0 else f"y{i}_{part}")
+                if part == 0:
+                    nc.scalar.copy(y[:], bank[:, span, :])
+                    (nc.scalar if last else nc.sync).dma_start(out=out_view[:, span, :], in_=y[:])
+                else:
+                    nc.vector.tensor_copy(y[:], bank[:, span, :])
+                    nc.sync.dma_start(out=out_view[:, span, :], in_=y[:])
+
+        row_scale(0)
+        row_scale(1)
+        pick(0)
+        turn(0)
+        row_scale(2)
+        pick(1)
+        turn(1)
+        pick(2)
+        turn(2)
+        row_scale(3)
+        pick(3)
+        second(0)
+        turn(3)
+        second(1)
+        second(2)
+        second(3)

@@ -30,6 +30,10 @@ def load_scales(queue, plane, rows, q):
     queue.dma_start(out=plane[32 * q : 32 * q + 32, :].bitcast(I32), in_=src)
 
 
+def load_scale_rows(queue, plane, rows, q):
+    queue.dma_start(out=plane[32 * q : 32 * q + 4, :].bitcast(I32), in_=rows[0, 4 * q : 4 * q + 4, :].bitcast(I32))
+
+
 def tile_list_unit_rows_listed_features_kernel(
     tc, xt_words, xt_scales, wc_words, wc_scales, fj, wo_words, wo_scales, offs, offs2, out
 ):
@@ -52,24 +56,22 @@ def tile_list_unit_rows_listed_features_kernel(
         warm = keep.tile([P, 2], F32, name="warm")
 
 
-        wc_flat = wc_words[0].rearrange("p n t -> p (n t)").bitcast(I32)
+        nc.vector.memset(wc_plane[:].bitcast(I32), 0)
+        nc.gpsimd.memset(warm[:, 0:1], 1.0)
+        nc.gpsimd.memset(wo_plane[:].bitcast(I32), 0)
         nc.sync.dma_start(token_list[:], offs2)
-        load_scales(nc.scalar, wc_plane, wc_scales, 0)
-        load_scales(nc.sync, x_plane, xt_scales, 0)
+        for q in range(4):
+            load_scales(nc.scalar if q % 2 == 0 else nc.sync, x_plane, xt_scales, q)
         nc.scalar.dma_start(out=x_words[:].bitcast(I32), in_=xt_words[0].bitcast(I32))
-        load_scales(nc.sync, x_plane, xt_scales, 1)
-        load_scales(nc.scalar, x_plane, xt_scales, 2)
-        load_scales(nc.sync, x_plane, xt_scales, 3)
-        nc.scalar.dma_start(out=wc_sb[:].bitcast(I32), in_=wc_flat)
-        for q in range(1, 4):
-            load_scales(nc.sync, wc_plane, wc_scales, q)
         nc.sync.dma_start(feature_list[:], offs)
+        nc.scalar.dma_start(out=wc_sb[:].bitcast(I32), in_=wc_words[0].rearrange("p n t -> p (n t)").bitcast(I32))
+        for q in range(4):
+            load_scale_rows(nc.sync, wc_plane, wc_scales, q)
         nc.sync.dma_start(out=fj_sb[:], in_=fj.rearrange("(p t) o -> p (t o)", t=PACK))
         nc.sync.dma_start(out=wo_sb[:].bitcast(I32), in_=wo_words[0].bitcast(I32))
         for q in range(4):
-            load_scales(nc.sync, wo_plane, wo_scales, q)
+            load_scale_rows(nc.sync, wo_plane, wo_scales, q)
 
-        nc.gpsimd.memset(warm[:, 0:1], 1.0)
         nc.scalar.activation(warm[:, 1:2], warm[:, 0:1], ACT.Abs_reciprocal_sqrt)
         make_identity(nc, ident[:])
 
@@ -103,24 +105,24 @@ def tile_list_unit_rows_listed_features_kernel(
         picked = {}
 
         def row_scale(i):
-            r = keep.tile([P, 1], F32, name=f"rstd{i}", tag=f"rstd{max(i - 1, 0)}")
-            stat = keep.tile([P, 4], F32, name=f"stat{i}", tag=f"stat{i % 2}")
+            r = keep.tile([P, 1], F32, name=f"rstd{i}", tag=f"rstd{i}")
+            sums = keep.tile([P, 3], F32, name=f"sums{i}", tag=f"sums{i % 2}")
             if i == 1:
-                moments = keep.tile([P, 16], F32, name="moments", tag="g0")
+                moments = keep.tile([P, 4, 3], F32, name="moments")
+                scrap = keep.tile([P, 2, 4], F32, name="scrap", tag="rstd0")
                 for h in range(2):
-                    nc.vector.bn_stats(moments[:, 6 * h : 6 * h + 6], z[i][h][:])
-                nc.vector.bn_aggr(moments[:, 12:14], moments[:, 0:12])
-                nc.vector.scalar_tensor_tensor(
-                    stat[:, 0:1], moments[:, 12:13], moments[:, 12:13], moments[:, 13:14], ALU.mult, ALU.add
+                    nc.vector.bn_stats(moments[:, 2 * h : 2 * h + 2, :].rearrange("p a b -> p (a b)"), z[i][h][:])
+                nc.scalar.activation(scrap[:, 0, :], moments[:, :, 1], ACT.Square, scale=0.5, accum_out=sums[:, 1:2])
+                nc.scalar.activation(
+                    scrap[:, 1, :], moments[:, :, 2], ACT.Identity, scale=1.0 / C, bias=EPS / 4, accum_out=sums[:, 2:3]
                 )
-                nc.scalar.activation(r[:], stat[:, 0:1], ACT.Abs_reciprocal_sqrt, bias=EPS)
             else:
                 for h in range(2):
                     nc.scalar.activation(
-                        u[i][:, halves[h]], z[i][h][:], ACT.Square, scale=1.0 / 32.0, accum_out=stat[:, h : h + 1]
+                        u[i][:, halves[h]], z[i][h][:], ACT.Square, scale=1.0 / 32.0, accum_out=sums[:, h : h + 1]
                     )
-                nc.scalar.activation(stat[:, 2:3], stat[:, 0:1], ACT.Identity, bias=EPS)
-                nc.scalar.activation(r[:], stat[:, 1:2], ACT.Abs_reciprocal_sqrt, bias=stat[:, 2:3])
+                nc.scalar.activation(sums[:, 2:3], sums[:, 0:1], ACT.Identity, bias=EPS)
+            nc.scalar.activation(r[:], sums[:, 1:2], ACT.Abs_reciprocal_sqrt, bias=sums[:, 2:3])
             rstd[i] = r
 
         def pick(i):
@@ -139,7 +141,7 @@ def tile_list_unit_rows_listed_features_kernel(
 
         def turn(i):
             g = picked[i]
-            pair = psum.tile([P, PACK, P], F32, name=f"t{i}", tag=f"bank{2 * i if i < TILES - 1 else 1}")
+            pair = psum.tile([P, PACK, P], F32, name=f"t{i}", tag=f"bank{2 * i}")
             by_slot = g[:].rearrange("p (q t) -> p t q", t=PACK)
             for t in range(PACK):
                 nc.tensor.transpose(pair[:, t, :], by_slot[:, t, :], ident[:])
@@ -147,7 +149,8 @@ def tile_list_unit_rows_listed_features_kernel(
 
         def second(i):
             pair = later[i]
-            uw = rows.tile([P, P, PACK], BF16, name=f"uw{i}", align_bytes=64, offset=4 * C * (i + 1))
+            place = [4 * C, 4 * C * 2, 4 * C * 3, 4 * C * 4][i]
+            uw = rows.tile([P, P, PACK], BF16, name=f"uw{i}", align_bytes=64, offset=place)
             nc.vector.tensor_tensor(
                 uw[:],
                 pair[:].rearrange("p t i -> p i t"),
@@ -164,12 +167,14 @@ def tile_list_unit_rows_listed_features_kernel(
             )
             last = i == TILES - 1
             out_view = out.rearrange("(a p) i -> p a i", p=P)[:, :, i * P : (i + 1) * P]
-            for part in range(2 if last else 1):
-                blocks = range(2 * part, 2 * part + 2) if last else range(4)
-                bank = psum.tile([P, PACK, P], F32, name=f"o{i}_{part}", tag=f"bank{2 * i + 1 - part}")
+            parts = 4 if last else 1
+            per = PACK // parts
+            for part in range(parts):
+                blocks = range(per * part, per * (part + 1))
+                bank = psum.tile([P, per, P], F32, name=f"o{i}_{part}", tag=f"bank{2 * i + 1 if part == 0 else 2 * (part - 1)}")
                 for a in blocks:
                     nc.tensor.matmul_mx(
-                        out=bank[:, a, :],
+                        out=bank[:, a - blocks.start, :],
                         lhsT=wo_sb[:, 2 * a * P : 2 * (a + 1) * P].bitcast(FP4X4),
                         lhsT_scale=wo_plane[:, a * P : (a + 1) * P],
                         rhs=codes[:].bitcast(FP8X4),
@@ -177,14 +182,13 @@ def tile_list_unit_rows_listed_features_kernel(
                         start=True,
                         stop=True,
                     )
-                span = slice(blocks.start, blocks.stop)
-                y = keep.tile([P, len(blocks), P], F32, name=f"y{i}_{part}", tag="rstd2" if i == 0 else f"y{i}_{part}")
-                if part == 0:
-                    nc.scalar.copy(y[:], bank[:, span, :])
-                    (nc.scalar if last else nc.sync).dma_start(out=out_view[:, span, :], in_=y[:])
+                y = keep.tile([P, per, P], F32, name=f"y{i}_{part}", tag="rstd3" if i == 0 else f"y{i}_{part}")
+                if part % 2 == 0:
+                    nc.scalar.copy(y[:], bank[:])
                 else:
-                    nc.vector.tensor_copy(y[:], bank[:, span, :])
-                    nc.sync.dma_start(out=out_view[:, span, :], in_=y[:])
+                    nc.vector.tensor_copy(y[:], bank[:])
+                queue = nc.scalar if (last and part == parts - 2) else nc.sync
+                queue.dma_start(out=out_view[:, blocks.start : blocks.stop, :], in_=y[:])
 
         row_scale(0)
         row_scale(1)
@@ -193,12 +197,12 @@ def tile_list_unit_rows_listed_features_kernel(
         row_scale(2)
         pick(1)
         turn(1)
+        row_scale(3)
         pick(2)
         turn(2)
-        row_scale(3)
         pick(3)
-        second(0)
         turn(3)
+        second(0)
         second(1)
         second(2)
         second(3)

@@ -167,11 +167,12 @@ def tile_list_unit_rows_listed_features_kernel(
             )
             last = i == TILES - 1
             out_view = out.rearrange("(a p) i -> p a i", p=P)[:, :, i * P : (i + 1) * P]
-            parts = 4 if last else 1
+            banks = [(1,), (3, 1), (5, 0), (7, 2, 4, 3)][i]
+            parts = len(banks)
             per = PACK // parts
             for part in range(parts):
                 blocks = range(per * part, per * (part + 1))
-                bank = psum.tile([P, per, P], F32, name=f"o{i}_{part}", tag=f"bank{2 * i + 1 if part == 0 else 2 * (part - 1)}")
+                bank = psum.tile([P, per, P], F32, name=f"o{i}_{part}", tag=f"bank{banks[part]}")
                 for a in blocks:
                     nc.tensor.matmul_mx(
                         out=bank[:, a - blocks.start, :],
@@ -183,7 +184,7 @@ def tile_list_unit_rows_listed_features_kernel(
                         stop=True,
                     )
                 y = keep.tile([P, per, P], F32, name=f"y{i}_{part}", tag="rstd3" if i == 0 else f"y{i}_{part}")
-                if part % 2 == 0:
+                if part % 2 == 0 or not last:
                     nc.scalar.copy(y[:], bank[:])
                 else:
                     nc.vector.tensor_copy(y[:], bank[:])

from contextlib import ExitStack

import concourse.mybir as mybir
from concourse.masks import make_identity

K, T, I, C, J, N = 512, 1024, 512, 1024, 512, 512
P = 128
PACK = 4
BANK = 512
TILES = I // P
EPS = 0.01

F32 = mybir.dt.float32
BF16 = mybir.dt.bfloat16
I32 = mybir.dt.int32
U32 = mybir.dt.uint32
U16 = mybir.dt.uint16
U8 = mybir.dt.uint8
FP8X4 = mybir.dt.float8_e4m3fn_x4
FP4X4 = mybir.dt.float4_e2m1fn_x4
ACT = mybir.ActivationFunctionType
ALU = mybir.AluOpType

FLOPS = 2 * K * I * C + 2 * J * N * I


def load_scales(queue, plane, rows, q):
    width = rows.shape[2] // 4
    src = rows[0, 4 * q : 4 * q + 4, :].bitcast(I32).unsqueeze(0).to_broadcast([8, 4, width])
    queue.dma_start(out=plane[32 * q : 32 * q + 32, :].bitcast(I32), in_=src)


def load_scale_rows(queue, plane, rows, q):
    queue.dma_start(out=plane[32 * q : 32 * q + 4, :].bitcast(I32), in_=rows[0, 4 * q : 4 * q + 4, :].bitcast(I32))


def tile_list_unit_rows_listed_features_kernel(
    tc, xt_words, xt_scales, wc_words, wc_scales, fj, wo_words, wo_scales, offs, offs2, out
):
    nc = tc.nc
    with ExitStack() as ctx:
        keep = ctx.enter_context(tc.tile_pool(name="keep", bufs=1))
        rows = ctx.enter_context(tc.tile_pool(name="rows", bufs=1))
        psum = ctx.enter_context(tc.psum_pool(name="psum", bufs=1))

        token_list = keep.tile([P, I // 16], U16, name="token_list")
        feature_list = keep.tile([P, J // 16], U16, name="feature_list")
        x_words = keep.tile([P, T], U16, name="x_words", align_bytes=64)
        x_plane = keep.tile([P, T], U8, name="x_plane", align_bytes=64)
        wc_sb = keep.tile([P, C], U32, name="wc_sb", align_bytes=64)
        wc_plane = keep.tile([P, C], U8, name="wc_plane", align_bytes=64)
        wo_sb = keep.tile([P, 2 * N], U8, name="wo_sb", align_bytes=64)
        wo_plane = keep.tile([P, N], U8, name="wo_plane", align_bytes=64)
        fj_sb = keep.tile([P, PACK], F32, name="fj_sb")
        ident = keep.tile([P, P], F32, name="ident")
        warm = keep.tile([P, 2], F32, name="warm")


        nc.vector.memset(wc_plane[:].bitcast(I32), 0)
        nc.gpsimd.memset(warm[:, 0:1], 1.0)
        nc.gpsimd.memset(wo_plane[:].bitcast(I32), 0)
        nc.sync.dma_start(token_list[:], offs2)
        for q in range(4):
            load_scales(nc.scalar if q % 2 == 0 else nc.sync, x_plane, xt_scales, q)
        nc.scalar.dma_start(out=x_words[:].bitcast(I32), in_=xt_words[0].bitcast(I32))
        nc.sync.dma_start(feature_list[:], offs)
        nc.scalar.dma_start(out=wc_sb[:].bitcast(I32), in_=wc_words[0].rearrange("p n t -> p (n t)").bitcast(I32))
        for q in range(4):
            load_scale_rows(nc.sync, wc_plane, wc_scales, q)
        nc.sync.dma_start(out=fj_sb[:], in_=fj.rearrange("(p t) o -> p (t o)", t=PACK))
        nc.sync.dma_start(out=wo_sb[:].bitcast(I32), in_=wo_words[0].bitcast(I32))
        for q in range(4):
            load_scale_rows(nc.sync, wo_plane, wo_scales, q)

        nc.scalar.activation(warm[:, 1:2], warm[:, 0:1], ACT.Abs_reciprocal_sqrt)
        make_identity(nc, ident[:])

        z = []
        for first, count in ((0, 1), (1, 1), (2, 2)):
            cols = slice(first * 8, (first + count) * 8)
            xg_words = keep.tile([P, count * P], U16, name=f"xg_words{first}", align_bytes=64)
            xg_plane = keep.tile([P, count * P], U8, name=f"xg_plane{first}", align_bytes=64)
            nc.vector.tensor_copy(xg_words[:], x_words[:].indirect(token_list[:, cols]))
            nc.vector.tensor_copy(xg_plane[:], x_plane[:].indirect(token_list[:, cols]))
            for s in range(count):
                pair = []
                for h in range(2):
                    bank = psum.tile([P, BANK], F32, name=f"z{first + s}{h}", tag=f"bank{2 * (first + s) + h}")
                    pair.append(bank)
                    nc.tensor.matmul_mx(
                        out=bank[:],
                        lhsT=xg_words[:, s * P : (s + 1) * P].bitcast(FP4X4),
                        lhsT_scale=xg_plane[:, s * P : (s + 1) * P],
                        rhs=wc_sb[:, h * BANK : (h + 1) * BANK].bitcast(FP8X4),
                        rhs_scale=wc_plane[:, h * BANK : (h + 1) * BANK],
                        start=True,
                        stop=True,
                    )
                z.append(pair)

        halves = [slice(h * BANK, (h + 1) * BANK) for h in range(2)]
        u = [rows.tile([P, C], F32, name=f"u{i}", align_bytes=64, offset=4 * C * i) for i in range(TILES)]
        rstd = {}
        later = {}
        picked = {}

        def row_scale(i):
            r = keep.tile([P, 1], F32, name=f"rstd{i}", tag=f"rstd{i}")
            sums = keep.tile([P, 3], F32, name=f"sums{i}", tag=f"sums{i % 2}")
            if i == 1:
                moments = keep.tile([P, 4, 3], F32, name="moments")
                scrap = keep.tile([P, 2, 4], F32, name="scrap", tag="rstd0")
                for h in range(2):
                    nc.vector.bn_stats(moments[:, 2 * h : 2 * h + 2, :].rearrange("p a b -> p (a b)"), z[i][h][:])
                nc.scalar.activation(scrap[:, 0, :], moments[:, :, 1], ACT.Square, scale=0.5, accum_out=sums[:, 1:2])
                nc.scalar.activation(
                    scrap[:, 1, :], moments[:, :, 2], ACT.Identity, scale=1.0 / C, bias=EPS / 4, accum_out=sums[:, 2:3]
                )
            else:
                for h in range(2):
                    nc.scalar.activation(
                        u[i][:, halves[h]], z[i][h][:], ACT.Square, scale=1.0 / 32.0, accum_out=sums[:, h : h + 1]
                    )
                nc.scalar.activation(sums[:, 2:3], sums[:, 0:1], ACT.Identity, bias=EPS)
            nc.scalar.activation(r[:], sums[:, 1:2], ACT.Abs_reciprocal_sqrt, bias=sums[:, 2:3])
            rstd[i] = r

        def pick(i):
            r = rstd[i]
            if i in (0, 1):
                nc.vector.tensor_scalar(u[i][:, halves[0]], z[i][0][:], r[:], None, ALU.mult)
                nc.scalar.activation(u[i][:, halves[1]], z[i][1][:], ACT.Copy, scale=r[:])
            elif True:
                for h in range(2):
                    nc.scalar.activation(u[i][:, halves[h]], z[i][h][:], ACT.Copy, scale=r[:])
            else:
                nc.scalar.activation(u[i][:], z[i][:], ACT.Copy, scale=r[:])
            g = keep.tile([P, J], F32, name=f"picked{i}", tag=f"g{i}")
            nc.vector.tensor_copy(g[:], u[i][:].indirect(feature_list[:]))
            picked[i] = g

        def turn(i):
            g = picked[i]
            pair = psum.tile([P, PACK, P], F32, name=f"t{i}", tag=f"bank{2 * i}")
            by_slot = g[:].rearrange("p (q t) -> p t q", t=PACK)
            for t in range(PACK):
                nc.tensor.transpose(pair[:, t, :], by_slot[:, t, :], ident[:])
            later[i] = pair

        def second(i):
            pair = later[i]
            place = [4 * C, 4 * C * 2, 4 * C * 3, 4 * C * 4][i]
            uw = rows.tile([P, P, PACK], BF16, name=f"uw{i}", align_bytes=64, offset=place)
            nc.vector.tensor_tensor(
                uw[:],
                pair[:].rearrange("p t i -> p i t"),
                fj_sb[:].unsqueeze(1).to_broadcast([P, P, PACK]),
                ALU.mult,
            )
            if i == 1:
                codes = rows.tile([P, P], U32, name="codes1", align_bytes=64, offset=4 * C * 3 + 2 * J)
            else:
                codes = keep.tile([P, P], U32, name=f"codes{i}", align_bytes=64)
            plane = keep.tile([P, P], U8, name=f"plane{i}", align_bytes=64)
            nc.vector.quantize_mx(
                out=codes[:].bitcast(FP8X4), scales=plane[:], in_=uw[:].rearrange("p i t -> p (i t)")
            )
            last = i == TILES - 1
            out_view = out.rearrange("(a p) i -> p a i", p=P)[:, :, i * P : (i + 1) * P]
            banks = [(1,), (3, 1), (5, 0), (7, 2, 4, 3)][i]
            parts = len(banks)
            per = PACK // parts
            for part in range(parts):
                blocks = range(per * part, per * (part + 1))
                bank = psum.tile([P, per, P], F32, name=f"o{i}_{part}", tag=f"bank{banks[part]}")
                for a in blocks:
                    nc.tensor.matmul_mx(
                        out=bank[:, a - blocks.start, :],
                        lhsT=wo_sb[:, 2 * a * P : 2 * (a + 1) * P].bitcast(FP4X4),
                        lhsT_scale=wo_plane[:, a * P : (a + 1) * P],
                        rhs=codes[:].bitcast(FP8X4),
                        rhs_scale=plane[:],
                        start=True,
                        stop=True,
                    )
                y = keep.tile([P, per, P], F32, name=f"y{i}_{part}", tag="rstd3" if i == 0 else f"y{i}_{part}")
                if part % 2 == 0 or not last:
                    nc.scalar.copy(y[:], bank[:])
                else:
                    nc.vector.tensor_copy(y[:], bank[:])
                queue = nc.scalar if (last and part == parts - 2) else nc.sync
                queue.dma_start(out=out_view[:, blocks.start : blocks.stop, :], in_=y[:])

        row_scale(0)
        row_scale(1)
        pick(0)
        turn(0)
        row_scale(2)
        pick(1)
        turn(1)
        row_scale(3)
        pick(2)
        turn(2)
        pick(3)
        turn(3)
        second(0)
        second(1)
        second(2)
        second(3)
